import numpy as np
import ml_dtypes


def mxq(x, axis, fmt="e4m3"):
    dtype, down = {"e4m3": (ml_dtypes.float8_e4m3fn, 7), "e5m2": (ml_dtypes.float8_e5m2, 14)}[fmt]
    v = np.moveaxis(np.asarray(x, np.float32).astype(ml_dtypes.bfloat16).astype(np.float64), axis, -1)
    blocks = v.reshape(v.shape[:-1] + (-1, 32))
    amax = np.abs(blocks).max(-1, keepdims=True)
    byte = np.maximum(np.where(amax > 0, np.frexp(amax)[1] - 1 + 127, 0) - down, 1)
    scale = np.exp2(byte - 127.0)
    codes = (blocks / scale).astype(np.float32).astype(dtype).astype(np.float64)
    return np.moveaxis((codes * scale).reshape(v.shape), -1, axis)


WIDE = False


def mx_kscale(k):
    if not WIDE:
        return np.ones(k)
    levels = np.array([10, -10, 5, -5, 0])
    if k % 512:
        return np.exp2(np.random.permutation(np.resize(levels, k // 32))).repeat(32)
    a = np.empty((k // 512, 16))
    for p in range(k // 512):
        a[p, :8] = np.random.permutation(np.resize(levels, 8))
        for g in range(8):
            far = levels[np.abs(levels - a[p, g]) >= 10]
            a[p, g + 8] = far[np.random.randint(len(far))]
    return np.exp2(a.ravel()).repeat(32)


def f64(x):
    return np.asarray(x).astype(np.float64)


def striped(idx):
    return np.tile(idx.reshape(-1, 16).T, (8, 1)).astype(np.uint16)


def unstriped(offs):
    return offs[:16].T.reshape(-1).astype(np.int64)


def pack_weight(w):
    k, n = w.shape
    w = f64(np.asarray(w, np.float32).astype(ml_dtypes.bfloat16)).reshape(k // 32, 32, n)
    amax = np.abs(w).max(1)
    byte = np.clip(np.where(amax > 0, np.frexp(amax)[1] - 1 + 127 - 7, 1), 1, 254)
    scaled = (w * np.exp2(127.0 - byte)[:, None, :]).reshape(k, n).astype(np.float32)
    words = np.ascontiguousarray(scaled.reshape(k // 512, 128, 4, n).transpose(0, 1, 3, 2)).astype(ml_dtypes.float8_e4m3fn).view(np.uint8)
    return words, np.ascontiguousarray(byte.astype(np.uint8).reshape(k // 512, 16, n))


def unpack_weight(words, scales):
    g, p, n, _ = words.shape
    vals = np.ascontiguousarray(words).view(ml_dtypes.float8_e4m3fn).astype(np.float64) * np.repeat(np.exp2(scales.astype(np.float64) - 127.0), 8, axis=1)[..., None]
    return vals.transpose(0, 1, 3, 2).reshape(g * 512, n)


def sigmoid(v):
    return 1.0 / (1.0 + np.exp(-np.maximum(v, -700.0)))


K, T, S, N, W, G = 512, 1024, 512, 128, 2048, 1024


def setup_inputs():
    n = np.random.standard_normal
    s = mx_kscale(K)[:, None]
    packed_xT = pack_weight(n((K, T)) * s)
    packed_eT = pack_weight(n((K, W)) * s)
    packed_dT = pack_weight(n((K, G)) * s)
    return {
        "x_words": packed_xT[0],
        "x_scales": packed_xT[1],
        "e_words": packed_eT[0],
        "e_scales": packed_eT[1],
        "d_words": packed_dT[0],
        "d_scales": packed_dT[1],
        "wui": (n((K, N)) / np.sqrt(K) / s).astype(np.float32),
        "wuc": (n((K, N)) / np.sqrt(K) / s).astype(np.float32),
        "wiu": (n((K, N)) / np.sqrt(K) / s).astype(np.float32),
        "wic": (n((K, N)) / np.sqrt(K) / s).astype(np.float32),
        "wcu": (n((K, N)) / np.sqrt(K) / s).astype(np.float32),
        "wci": (n((K, N)) / np.sqrt(K) / s).astype(np.float32),
        "offs": striped(np.random.permutation(T)[:S]),
        "item": striped(np.random.permutation(W)[:S]),
        "cxt": striped(np.random.permutation(G)[:S]),
    }


def reference(x_words, x_scales, e_words, e_scales, d_words, d_scales, wui, wuc, wiu, wic, wcu, wci, offs, item, cxt):
    xq = unpack_weight(x_words, x_scales)[:, unstriped(offs)]
    yui = mxq(f64(wui), 0, "e4m3").T @ xq
    e_item = unpack_weight(e_words, e_scales)[:, unstriped(item)]
    yiu = mxq(f64(wiu), 0, "e4m3").T @ e_item
    yuc = mxq(f64(wuc), 0, "e4m3").T @ xq
    d_cxt = unpack_weight(d_words, d_scales)[:, unstriped(cxt)]
    ycu = mxq(f64(wcu), 0, "e4m3").T @ d_cxt
    yic = mxq(f64(wic), 0, "e4m3").T @ e_item
    yci = mxq(f64(wci), 0, "e4m3").T @ d_cxt
    return sigmoid(yui * yiu + yuc * ycu + yic * yci)

@@ -1,0 +1,171 @@
+from contextlib import ExitStack
+
+import concourse.mybir as mybir
+from concourse.masks import make_identity
+
+K, S, N = 512, 512, 128
+FLOPS = 6 * 2 * K * N * S
+
+F32 = mybir.dt.float32
+BF16 = mybir.dt.bfloat16
+I32 = mybir.dt.int32
+U32 = mybir.dt.uint32
+U16 = mybir.dt.uint16
+U8 = mybir.dt.uint8
+FP8X4 = mybir.dt.float8_e4m3fn_x4
+MULT = mybir.AluOpType.mult
+SIGMOID = mybir.ActivationFunctionType.Sigmoid
+
+P = 128
+PACK = 4
+CHUNK = 128
+CHUNKS = S // CHUNK
+HALF = S // 2
+
+
+def tile_picked_yffm_sig_p_kernel(
+    tc, x_words, x_scales, e_words, e_scales, d_words, d_scales,
+    wui, wuc, wiu, wic, wcu, wci, offs, item, cxt, out,
+):
+    nc = tc.nc
+    with ExitStack() as ctx:
+        keep = ctx.enter_context(tc.tile_pool(name="keep", bufs=1))
+        psum = ctx.enter_context(tc.psum_pool(name="psum", bufs=1))
+
+        def scale_window(name, scales):
+            window = keep.tile([P, scales.shape[2]], U8, name=name, align_bytes=64)
+            nc.vector.memset(window[:].bitcast(I32), 0)
+            return window
+
+        def load_scales(queue, window, scales):
+            rows = scales[0].bitcast(I32).rearrange("(q r) c -> r q c", r=PACK)
+            for r in range(PACK):
+                queue.dma_start(out=window[r:P:32, :].bitcast(I32), in_=rows[r])
+
+        def load_list(name, entries):
+            tile = keep.tile([P, S // 16], U16, name=name)
+            nc.sync.dma_start(tile[:], entries)
+            return tile
+
+        def load_words(name, words):
+            window = keep.tile([P, words.shape[2]], I32, name=name, align_bytes=64)
+            nc.sync.dma_start(out=window[:], in_=words[0].rearrange("p c t -> p (c t)").bitcast(I32))
+            return window
+
+        def load_weight(name, w):
+            raw = keep.tile([P, PACK, N], F32, name=name, align_bytes=64)
+            nc.sync.dma_start(out=raw[:], in_=w.rearrange("(p t) n -> p t n", t=PACK))
+            return raw
+
+        def gather(name, dtype, window, offsets, first, count):
+            picked = keep.tile([P, count], dtype, name=name, align_bytes=64)
+            nc.vector.tensor_copy(
+                picked[:], window[:].bitcast(dtype).indirect(offsets[:, first // 16 : (first + count) // 16])
+            )
+            return picked
+
+        def round_pair(name, raw_a, raw_b):
+            grouped = keep.tile([P, 2, N, PACK], BF16, name=name, align_bytes=64)
+            for i, raw in enumerate((raw_a, raw_b)):
+                nc.scalar.copy(out=grouped[:, i], in_=raw[:].rearrange("p t n -> p n t"))
+            return grouped
+
+        def quantize_pair(name, grouped):
+            codes = keep.tile([P, 2 * N], U32, name=name + "_codes", align_bytes=64)
+            planes = keep.tile([P, 2 * N], U8, name=name + "_scales", align_bytes=64)
+            nc.vector.quantize_mx(
+                out=codes[:].bitcast(FP8X4), scales=planes[:], in_=grouped[:].rearrange("p i n t -> p (i n t)")
+            )
+            return codes, planes
+
+        def project(dst, words, word0, scales, scale0, weights, cols):
+            codes, planes = weights
+            nc.tensor.matmul_mx(
+                out=dst,
+                lhsT=words[:, word0 : word0 + CHUNK].bitcast(FP8X4),
+                lhsT_scale=scales[:, scale0 : scale0 + CHUNK],
+                rhs=codes[:, cols].bitcast(FP8X4),
+                rhs_scale=planes[:, cols],
+                start=True,
+                stop=True,
+            )
+
+        xs_win = scale_window("xs_win", x_scales)
+        es_win = scale_window("es_win", e_scales)
+        ds_win = scale_window("ds_win", d_scales)
+
+        warm = keep.tile([P, 1], F32, name="warm")
+        nc.gpsimd.memset(warm[:], 0.0)
+        nc.scalar.activation(out=warm[:], in_=warm[:], func=SIGMOID)
+
+        x_list = load_list("x_list", offs)
+        load_scales(nc.sync, xs_win, x_scales)
+        xw_win = load_words("xw_win", x_words)
+        e_list = load_list("e_list", item)
+        raw_ui = load_weight("raw_ui", wui)
+        load_scales(nc.scalar, es_win, e_scales)
+        ew_win = load_words("ew_win", e_words)
+        d_list = load_list("d_list", cxt)
+        raw_uc = load_weight("raw_uc", wuc)
+        raw_iu = load_weight("raw_iu", wiu)
+        load_scales(nc.scalar, ds_win, d_scales)
+        raw_ic = load_weight("raw_ic", wic)
+        raw_cu = load_weight("raw_cu", wcu)
+        raw_ci = load_weight("raw_ci", wci)
+        dw_win = load_words("dw_win", d_words)
+
+        ident = keep.tile([P, P], F32, name="ident")
+        make_identity(nc, ident[:])
+
+        xs = gather("xs", U8, xs_win, x_list, 0, S)
+        xw = gather("xw", U32, xw_win, x_list, 0, S)
+        es = gather("es", U8, es_win, e_list, 0, S)
+        ds = gather("ds", U8, ds_win, d_list, 0, S)
+        ew = gather("ew", U32, ew_win, e_list, 0, S)
+
+        held = keep.tile([P, CHUNKS, 3 * N], F32, name="held", align_bytes=64)
+
+        w_x = quantize_pair("w_x", round_pair("g_x", raw_ui, raw_uc))
+        for h in range(2):
+            bank = psum.tile([P, 2, 2 * N], F32, name="x_bank", tag="bank%d" % h)
+            for i in range(2):
+                first = (2 * h + i) * CHUNK
+                project(bank[:, i], xw, first, xs, first, w_x, slice(0, 2 * N))
+            nc.scalar.copy(out=held[:, 2 * h : 2 * h + 2, 0 : 2 * N], in_=bank[:])
+
+        w_e = quantize_pair("w_e", round_pair("g_e", raw_iu, raw_ic))
+        iu_bank = psum.tile([P, CHUNKS, N], F32, name="iu_bank")
+        ic_bank = psum.tile([P, CHUNKS, N], F32, name="ic_bank")
+        for bank, cols in ((ic_bank, slice(N, 2 * N)), (iu_bank, slice(0, N))):
+            for c in range(CHUNKS):
+                project(bank[:, c], ew, c * CHUNK, es, c * CHUNK, w_e, cols)
+        nc.scalar.copy(out=held[:, :, 2 * N : 3 * N], in_=ic_bank[:])
+
+        w_d = quantize_pair("w_d", round_pair("g_d", raw_cu, raw_ci))
+
+        prod_ui = keep.tile([P, CHUNKS, N], F32, name="prod_ui", align_bytes=64)
+        nc.vector.tensor_tensor(prod_ui[:], iu_bank[:], held[:, :, 0:N], MULT)
+        sums = []
+        for c in range(CHUNKS):
+            total = psum.tile([P, CHUNK], F32, name="total", tag="bank%d" % c)
+            nc.tensor.matmul(total[:], lhsT=prod_ui[:, c], rhs=ident[:], is_transpose=True, start=True, stop=False)
+            sums.append(total)
+
+        d_banks = []
+        for h in range(2):
+            dw = gather("dw%d" % h, U32, dw_win, d_list, h * HALF, HALF)
+            bank = psum.tile([P, 2, 2 * N], F32, name="d_bank%d" % h)
+            for i in range(2):
+                project(bank[:, i], dw, i * CHUNK, ds, (2 * h + i) * CHUNK, w_d, slice(0, 2 * N))
+            d_banks.append(bank)
+
+        for h in range(2):
+            prod = keep.tile([P, 2, 2 * N], F32, name="prod%d" % h, align_bytes=64)
+            nc.vector.tensor_tensor(prod[:], d_banks[h][:], held[:, 2 * h : 2 * h + 2, N : 3 * N], MULT)
+            result = keep.tile([P, HALF], F32, name="result%d" % h, align_bytes=64)
+            for i in range(2):
+                total = sums[2 * h + i]
+                nc.tensor.matmul(total[:], lhsT=prod[:, i, 0:N], rhs=ident[:], is_transpose=True, start=False, stop=False)
+                nc.tensor.matmul(total[:], lhsT=prod[:, i, N : 2 * N], rhs=ident[:], is_transpose=True, start=False, stop=True)
+                nc.scalar.activation(out=result[:, i * CHUNK : (i + 1) * CHUNK], in_=total[:], func=SIGMOID)
+            nc.sync.dma_start(out=out[:, h * HALF : (h + 1) * HALF], in_=result[:])

@@ -33,7 +33,7 @@ def tile_picked_yffm_sig_p_kernel(
         psum = ctx.enter_context(tc.psum_pool(name="psum", bufs=1))
 
         def scale_window(name, scales):
-            window = keep.tile([P, scales.shape[2]], U8, name=name, align_bytes=64)
+            window = keep.tile([P, scales.shape[2]], U8, name=name, tag=name, align_bytes=64)
             nc.vector.memset(window[:].bitcast(I32), 0)
             return window
 
@@ -53,7 +53,7 @@ def tile_picked_yffm_sig_p_kernel(
             return window
 
         def load_weight(name, w):
-            raw = keep.tile([P, PACK, N], F32, name=name, align_bytes=64)
+            raw = keep.tile([P, PACK, N], F32, name=name, tag=name, align_bytes=64)
             nc.sync.dma_start(out=raw[:], in_=w.rearrange("(p t) n -> p t n", t=PACK))
             return raw
 
@@ -65,13 +65,13 @@ def tile_picked_yffm_sig_p_kernel(
             return picked
 
         def round_pair(name, raw_a, raw_b):
-            grouped = keep.tile([P, 2, N, PACK], BF16, name=name, align_bytes=64)
+            grouped = keep.tile([P, 2, N, PACK], BF16, name=name, tag=name, align_bytes=64)
             for i, raw in enumerate((raw_a, raw_b)):
                 nc.scalar.copy(out=grouped[:, i], in_=raw[:].rearrange("p t n -> p n t"))
             return grouped
 
-        def quantize_pair(name, grouped):
-            codes = keep.tile([P, 2 * N], U32, name=name + "_codes", align_bytes=64)
+        def quantize_pair(name, grouped, tag):
+            codes = keep.tile([P, 2 * N], U32, name=name + "_codes", tag=tag, align_bytes=64)
             planes = keep.tile([P, 2 * N], U8, name=name + "_scales", align_bytes=64)
             nc.vector.quantize_mx(
                 out=codes[:].bitcast(FP8X4), scales=planes[:], in_=grouped[:].rearrange("p i n t -> p (i n t)")
@@ -91,81 +91,87 @@ def tile_picked_yffm_sig_p_kernel(
             )
 
         xs_win = scale_window("xs_win", x_scales)
-        es_win = scale_window("es_win", e_scales)
         ds_win = scale_window("ds_win", d_scales)
+        es_win = scale_window("es_win", e_scales)
 
         warm = keep.tile([P, 1], F32, name="warm")
         nc.gpsimd.memset(warm[:], 0.0)
         nc.scalar.activation(out=warm[:], in_=warm[:], func=SIGMOID)
 
         x_list = load_list("x_list", offs)
-        load_scales(nc.sync, xs_win, x_scales)
         xw_win = load_words("xw_win", x_words)
-        e_list = load_list("e_list", item)
-        raw_ui = load_weight("raw_ui", wui)
-        load_scales(nc.scalar, es_win, e_scales)
-        ew_win = load_words("ew_win", e_words)
+        load_scales(nc.sync, xs_win, x_scales)
         d_list = load_list("d_list", cxt)
+        dw_win = load_words("dw_win", d_words)
         raw_uc = load_weight("raw_uc", wuc)
-        raw_iu = load_weight("raw_iu", wiu)
-        load_scales(nc.scalar, ds_win, d_scales)
-        raw_ic = load_weight("raw_ic", wic)
+        raw_ui = load_weight("raw_ui", wui)
+        load_scales(nc.sync, ds_win, d_scales)
         raw_cu = load_weight("raw_cu", wcu)
         raw_ci = load_weight("raw_ci", wci)
-        dw_win = load_words("dw_win", d_words)
+        raw_iu = load_weight("raw_iu", wiu)
+        raw_ic = load_weight("raw_ic", wic)
+        e_list = load_list("e_list", item)
+        load_scales(nc.sync, es_win, e_scales)
+        ew_win = load_words("ew_win", e_words)
 
         ident = keep.tile([P, P], F32, name="ident")
         make_identity(nc, ident[:])
 
-        xs = gather("xs", U8, xs_win, x_list, 0, S)
         xw = gather("xw", U32, xw_win, x_list, 0, S)
-        es = gather("es", U8, es_win, e_list, 0, S)
+        xs = gather("xs", U8, xs_win, x_list, 0, S)
+        dw = gather("dw", U32, dw_win, d_list, 0, S)
         ds = gather("ds", U8, ds_win, d_list, 0, S)
-        ew = gather("ew", U32, ew_win, e_list, 0, S)
 
-        held = keep.tile([P, CHUNKS, 3 * N], F32, name="held", align_bytes=64)
+        g_x = round_pair("g_x", raw_uc, raw_ui)
+        g_d = round_pair("g_d", raw_cu, raw_ci)
+        g_e = round_pair("g_e", raw_iu, raw_ic)
+        held = keep.tile([P, 3, CHUNKS, N], F32, name="held", tag="raw_ic", align_bytes=64)
 
-        w_x = quantize_pair("w_x", round_pair("g_x", raw_ui, raw_uc))
+        w_x = quantize_pair("w_x", g_x, "w_x")
         for h in range(2):
             bank = psum.tile([P, 2, 2 * N], F32, name="x_bank", tag="bank%d" % h)
             for i in range(2):
                 first = (2 * h + i) * CHUNK
                 project(bank[:, i], xw, first, xs, first, w_x, slice(0, 2 * N))
-            nc.scalar.copy(out=held[:, 2 * h : 2 * h + 2, 0 : 2 * N], in_=bank[:])
+            nc.scalar.copy(
+                out=held[:, 0:2, 2 * h : 2 * h + 2, :], in_=bank[:].rearrange("p c (j n) -> p j c n", j=2)
+            )
 
-        w_e = quantize_pair("w_e", round_pair("g_e", raw_iu, raw_ic))
-        iu_bank = psum.tile([P, CHUNKS, N], F32, name="iu_bank")
-        ic_bank = psum.tile([P, CHUNKS, N], F32, name="ic_bank")
-        for bank, cols in ((ic_bank, slice(N, 2 * N)), (iu_bank, slice(0, N))):
+        w_d = quantize_pair("w_d", g_d, "w_d")
+        cu_bank = psum.tile([P, CHUNKS, N], F32, name="cu_bank")
+        ci_bank = psum.tile([P, CHUNKS, N], F32, name="ci_bank")
+        for bank, cols in ((cu_bank, slice(0, N)), (ci_bank, slice(N, 2 * N))):
             for c in range(CHUNKS):
-                project(bank[:, c], ew, c * CHUNK, es, c * CHUNK, w_e, cols)
-        nc.scalar.copy(out=held[:, :, 2 * N : 3 * N], in_=ic_bank[:])
+                project(bank[:, c], dw, c * CHUNK, ds, c * CHUNK, w_d, cols)
+        nc.scalar.copy(out=held[:, 2], in_=ci_bank[:])
 
-        w_d = quantize_pair("w_d", round_pair("g_d", raw_cu, raw_ci))
+        es = gather("es", U8, es_win, e_list, 0, S)
+        w_e = quantize_pair("w_e", g_e, "es_win")
 
-        prod_ui = keep.tile([P, CHUNKS, N], F32, name="prod_ui", align_bytes=64)
-        nc.vector.tensor_tensor(prod_ui[:], iu_bank[:], held[:, :, 0:N], MULT)
+        prod_uc = keep.tile([P, CHUNKS, N], F32, name="prod_uc", tag="g_e", align_bytes=64)
+        nc.vector.tensor_tensor(prod_uc[:], cu_bank[:], held[:, 0], MULT)
         sums = []
         for c in range(CHUNKS):
             total = psum.tile([P, CHUNK], F32, name="total", tag="bank%d" % c)
-            nc.tensor.matmul(total[:], lhsT=prod_ui[:, c], rhs=ident[:], is_transpose=True, start=True, stop=False)
+            nc.tensor.matmul(total[:], lhsT=prod_uc[:, c], rhs=ident[:], is_transpose=True, start=True, stop=False)
             sums.append(total)
 
-        d_banks = []
+        e_banks = []
         for h in range(2):
-            dw = gather("dw%d" % h, U32, dw_win, d_list, h * HALF, HALF)
-            bank = psum.tile([P, 2, 2 * N], F32, name="d_bank%d" % h)
+            ew = gather("ew%d" % h, U32, ew_win, e_list, h * HALF, HALF)
+            bank = psum.tile([P, 2, 2 * N], F32, name="e_bank%d" % h)
             for i in range(2):
-                project(bank[:, i], dw, i * CHUNK, ds, (2 * h + i) * CHUNK, w_d, slice(0, 2 * N))
-            d_banks.append(bank)
+                project(bank[:, i], ew, i * CHUNK, es, (2 * h + i) * CHUNK, w_e, slice(0, 2 * N))
+            e_banks.append(bank)
 
-        for h in range(2):
-            prod = keep.tile([P, 2, 2 * N], F32, name="prod%d" % h, align_bytes=64)
-            nc.vector.tensor_tensor(prod[:], d_banks[h][:], held[:, 2 * h : 2 * h + 2, N : 3 * N], MULT)
-            result = keep.tile([P, HALF], F32, name="result%d" % h, align_bytes=64)
-            for i in range(2):
-                total = sums[2 * h + i]
-                nc.tensor.matmul(total[:], lhsT=prod[:, i, 0:N], rhs=ident[:], is_transpose=True, start=False, stop=False)
-                nc.tensor.matmul(total[:], lhsT=prod[:, i, N : 2 * N], rhs=ident[:], is_transpose=True, start=False, stop=True)
-                nc.scalar.activation(out=result[:, i * CHUNK : (i + 1) * CHUNK], in_=total[:], func=SIGMOID)
-            nc.sync.dma_start(out=out[:, h * HALF : (h + 1) * HALF], in_=result[:])
+        for c in range(CHUNKS):
+            prod = keep.tile([P, 2, N], F32, name="prod%d" % c, align_bytes=64)
+            nc.vector.tensor_tensor(
+                prod[:], e_banks[c // 2][:, c % 2].rearrange("p (j n) -> p j n", j=2), held[:, 1:3, c, :], MULT
+            )
+            total = sums[c]
+            nc.tensor.matmul(total[:], lhsT=prod[:, 0], rhs=ident[:], is_transpose=True, start=False, stop=False)
+            nc.tensor.matmul(total[:], lhsT=prod[:, 1], rhs=ident[:], is_transpose=True, start=False, stop=True)
+            result = keep.tile([P, CHUNK], F32, name="result%d" % c, align_bytes=64)
+            nc.scalar.activation(out=result[:], in_=total[:], func=SIGMOID)
+            nc.sync.dma_start(out=out[:, c * CHUNK : (c + 1) * CHUNK], in_=result[:])

from contextlib import ExitStack

import concourse.mybir as mybir
from concourse.masks import make_identity

K, S, N = 512, 512, 128
FLOPS = 6 * 2 * K * N * S

F32 = mybir.dt.float32
BF16 = mybir.dt.bfloat16
I32 = mybir.dt.int32
U32 = mybir.dt.uint32
U16 = mybir.dt.uint16
U8 = mybir.dt.uint8
FP8X4 = mybir.dt.float8_e4m3fn_x4
MULT = mybir.AluOpType.mult
SIGMOID = mybir.ActivationFunctionType.Sigmoid

P = 128
PACK = 4
CHUNK = 128
CHUNKS = S // CHUNK
HALF = S // 2


def tile_picked_yffm_sig_p_kernel(
    tc, x_words, x_scales, e_words, e_scales, d_words, d_scales,
    wui, wuc, wiu, wic, wcu, wci, offs, item, cxt, out,
):
    nc = tc.nc
    with ExitStack() as ctx:
        keep = ctx.enter_context(tc.tile_pool(name="keep", bufs=1))
        psum = ctx.enter_context(tc.psum_pool(name="psum", bufs=1))

        def scale_window(name, scales):
            window = keep.tile([P, scales.shape[2]], U8, name=name, tag=name, align_bytes=64)
            nc.vector.memset(window[:].bitcast(I32), 0)
            return window

        def load_scales(queue, window, scales):
            rows = scales[0].bitcast(I32).rearrange("(q r) c -> r q c", r=PACK)
            for r in range(PACK):
                queue.dma_start(out=window[r:P:32, :].bitcast(I32), in_=rows[r])

        def load_list(name, entries):
            tile = keep.tile([P, S // 16], U16, name=name)
            nc.sync.dma_start(tile[:], entries)
            return tile

        def load_words(name, words):
            window = keep.tile([P, words.shape[2]], I32, name=name, align_bytes=64)
            nc.sync.dma_start(out=window[:], in_=words[0].rearrange("p c t -> p (c t)").bitcast(I32))
            return window

        def load_weight(name, w):
            raw = keep.tile([P, PACK, N], F32, name=name, tag=name, align_bytes=64)
            nc.sync.dma_start(out=raw[:], in_=w.rearrange("(p t) n -> p t n", t=PACK))
            return raw

        def gather(name, dtype, window, offsets, first, count):
            picked = keep.tile([P, count], dtype, name=name, align_bytes=64)
            nc.vector.tensor_copy(
                picked[:], window[:].bitcast(dtype).indirect(offsets[:, first // 16 : (first + count) // 16])
            )
            return picked

        def round_pair(name, raw_a, raw_b):
            grouped = keep.tile([P, 2, N, PACK], BF16, name=name, tag=name, align_bytes=64)
            for i, raw in enumerate((raw_a, raw_b)):
                nc.scalar.copy(out=grouped[:, i], in_=raw[:].rearrange("p t n -> p n t"))
            return grouped

        def quantize_pair(name, grouped, tag):
            codes = keep.tile([P, 2 * N], U32, name=name + "_codes", tag=tag, align_bytes=64)
            planes = keep.tile([P, 2 * N], U8, name=name + "_scales", align_bytes=64)
            nc.vector.quantize_mx(
                out=codes[:].bitcast(FP8X4), scales=planes[:], in_=grouped[:].rearrange("p i n t -> p (i n t)")
            )
            return codes, planes

        def project(dst, words, word0, scales, scale0, weights, cols):
            codes, planes = weights
            nc.tensor.matmul_mx(
                out=dst,
                lhsT=words[:, word0 : word0 + CHUNK].bitcast(FP8X4),
                lhsT_scale=scales[:, scale0 : scale0 + CHUNK],
                rhs=codes[:, cols].bitcast(FP8X4),
                rhs_scale=planes[:, cols],
                start=True,
                stop=True,
            )

        xs_win = scale_window("xs_win", x_scales)
        ds_win = scale_window("ds_win", d_scales)
        es_win = scale_window("es_win", e_scales)

        warm = keep.tile([P, 1], F32, name="warm")
        nc.gpsimd.memset(warm[:], 0.0)
        nc.scalar.activation(out=warm[:], in_=warm[:], func=SIGMOID)

        x_list = load_list("x_list", offs)
        xw_win = load_words("xw_win", x_words)
        load_scales(nc.sync, xs_win, x_scales)
        d_list = load_list("d_list", cxt)
        dw_win = load_words("dw_win", d_words)
        raw_uc = load_weight("raw_uc", wuc)
        raw_ui = load_weight("raw_ui", wui)
        load_scales(nc.sync, ds_win, d_scales)
        raw_cu = load_weight("raw_cu", wcu)
        raw_ci = load_weight("raw_ci", wci)
        raw_iu = load_weight("raw_iu", wiu)
        raw_ic = load_weight("raw_ic", wic)
        e_list = load_list("e_list", item)
        load_scales(nc.sync, es_win, e_scales)
        ew_win = load_words("ew_win", e_words)

        ident = keep.tile([P, P], F32, name="ident")
        make_identity(nc, ident[:])

        xw = gather("xw", U32, xw_win, x_list, 0, S)
        xs = gather("xs", U8, xs_win, x_list, 0, S)
        dw = gather("dw", U32, dw_win, d_list, 0, S)
        ds = gather("ds", U8, ds_win, d_list, 0, S)

        g_x = round_pair("g_x", raw_uc, raw_ui)
        g_d = round_pair("g_d", raw_cu, raw_ci)
        g_e = round_pair("g_e", raw_iu, raw_ic)
        held = keep.tile([P, 3, CHUNKS, N], F32, name="held", tag="raw_ic", align_bytes=64)

        w_x = quantize_pair("w_x", g_x, "w_x")
        for h in range(2):
            bank = psum.tile([P, 2, 2 * N], F32, name="x_bank", tag="bank%d" % h)
            for i in range(2):
                first = (2 * h + i) * CHUNK
                project(bank[:, i], xw, first, xs, first, w_x, slice(0, 2 * N))
            nc.scalar.copy(
                out=held[:, 0:2, 2 * h : 2 * h + 2, :], in_=bank[:].rearrange("p c (j n) -> p j c n", j=2)
            )

        w_d = quantize_pair("w_d", g_d, "w_d")
        cu_bank = psum.tile([P, CHUNKS, N], F32, name="cu_bank")
        ci_bank = psum.tile([P, CHUNKS, N], F32, name="ci_bank")
        for bank, cols in ((cu_bank, slice(0, N)), (ci_bank, slice(N, 2 * N))):
            for c in range(CHUNKS):
                project(bank[:, c], dw, c * CHUNK, ds, c * CHUNK, w_d, cols)
        nc.scalar.copy(out=held[:, 2], in_=ci_bank[:])

        es = gather("es", U8, es_win, e_list, 0, S)
        w_e = quantize_pair("w_e", g_e, "es_win")

        prod_uc = keep.tile([P, CHUNKS, N], F32, name="prod_uc", tag="g_e", align_bytes=64)
        nc.vector.tensor_tensor(prod_uc[:], cu_bank[:], held[:, 0], MULT)
        sums = []
        for c in range(CHUNKS):
            total = psum.tile([P, CHUNK], F32, name="total", tag="bank%d" % c)
            nc.tensor.matmul(total[:], lhsT=prod_uc[:, c], rhs=ident[:], is_transpose=True, start=True, stop=False)
            sums.append(total)

        e_banks = []
        for h in range(2):
            ew = gather("ew%d" % h, U32, ew_win, e_list, h * HALF, HALF)
            bank = psum.tile([P, 2, 2 * N], F32, name="e_bank%d" % h)
            for i in range(2):
                project(bank[:, i], ew, i * CHUNK, es, (2 * h + i) * CHUNK, w_e, slice(0, 2 * N))
            e_banks.append(bank)

        for c in range(CHUNKS):
            prod = keep.tile([P, 2, N], F32, name="prod%d" % c, align_bytes=64)
            nc.vector.tensor_tensor(
                prod[:], e_banks[c // 2][:, c % 2].rearrange("p (j n) -> p j n", j=2), held[:, 1:3, c, :], MULT
            )
            total = sums[c]
            nc.tensor.matmul(total[:], lhsT=prod[:, 0], rhs=ident[:], is_transpose=True, start=False, stop=False)
            nc.tensor.matmul(total[:], lhsT=prod[:, 1], rhs=ident[:], is_transpose=True, start=False, stop=True)
            result = keep.tile([P, CHUNK], F32, name="result%d" % c, align_bytes=64)
            nc.scalar.activation(out=result[:], in_=total[:], func=SIGMOID)
            nc.sync.dma_start(out=out[:, c * CHUNK : (c + 1) * CHUNK], in_=result[:])
